import numpy as np
import ml_dtypes

BF16 = ml_dtypes.bfloat16


def bf(x):
    return np.asarray(x, np.float32).astype(BF16)


def f32(x):
    return np.asarray(x, np.float32)


def f64(x):
    return np.asarray(x).astype(np.float64)


def striped(idx):
    return np.tile(idx.reshape(-1, 16).T, (8, 1))


S, K, M, N, E, Q = 1024, 128, 128, 2048, 4, 512


def two_experts():
    first = np.random.permutation(S).reshape(E, S // E)
    return np.concatenate([np.random.permutation(np.concatenate([first[e], first[(e + 1) % E]])) for e in range(E)])


def setup_inputs():
    return {"table": bf(np.random.standard_normal((S, K))), "w": bf(np.random.standard_normal((E, K, M)) / np.sqrt(K)), "b": f32(0.5 * np.random.standard_normal((M, 1))), "offs": striped(two_experts())}


def reference(table, w, b, offs):
    idx = offs[:16].T.reshape(-1)
    x = f64(table)[idx].T
    y = np.concatenate([f64(w)[e].T @ x[:, e * Q : (e + 1) * Q] for e in range(E)], axis=1)
    return np.maximum(y + f64(b), 0.0)

@@ -1,0 +1,56 @@
+import concourse.mybir as mybir
+from concourse.masks import make_identity
+
+BF16, F32, U16 = mybir.dt.bfloat16, mybir.dt.float32, mybir.dt.uint16
+ADD, MAX = mybir.AluOpType.add, mybir.AluOpType.max
+RELU = mybir.ActivationFunctionType.Relu
+
+P = 128
+TOKENS = 1024
+BLOCKS = TOKENS // P
+EXPERTS = 4
+PIECE = 512
+PIECE_COLS = PIECE // 16
+HALF = TOKENS // 2
+
+FLOPS = 2 * P * P * EXPERTS * PIECE
+
+
+def tile_gather_matmul_kernel(tc, table, w, b, offs, out):
+    nc = tc.nc
+    with (
+        tc.tile_pool(name="held", bufs=1) as held,
+        tc.psum_pool(name="flip", bufs=1) as flip,
+        tc.psum_pool(name="product", bufs=1) as product,
+    ):
+        offsets = held.tile([P, EXPERTS * PIECE_COLS], U16, name="offsets")
+        nc.sync.dma_start(offsets[:], offs)
+        rows = held.tile([P, BLOCKS, P], BF16, name="rows")
+        nc.scalar.dma_start(rows[:], table.rearrange("(a p) k -> p a k", p=P))
+        weights = held.tile([P, EXPERTS, P], BF16, name="weights")
+        nc.sync.dma_start(weights[:], w.rearrange("e k m -> k e m"))
+        bias = held.tile([P, 1], F32, name="bias")
+        nc.sync.dma_start(bias[:], b)
+
+        identity = held.tile([P, P], BF16, name="identity")
+        make_identity(nc, identity[:])
+
+        window = held.tile([P, TOKENS], BF16, name="window")
+        flipped = [flip.tile([P, HALF], BF16, name=f"flipped{h}") for h in range(2)]
+        for a in range(BLOCKS):
+            h, col = divmod(a * P, HALF)
+            nc.tensor.transpose(flipped[h][:, col : col + P], rows[:, a, :], identity[:])
+        nc.vector.tensor_copy(window[:, 0:HALF], flipped[0][:])
+        nc.scalar.copy(window[:, HALF:TOKENS], flipped[1][:])
+
+        for e in range(EXPERTS):
+            bank = product.tile([P, PIECE], F32, name=f"bank{e}")
+            picked = window[:].indirect(offsets[:, e * PIECE_COLS : (e + 1) * PIECE_COLS])
+            nc.tensor.matmul(bank[:], weights[:, e, :], picked, start=True, stop=True)
+            result = held.tile([P, PIECE], F32, name=f"result{e}")
+            if e % 2 == 0:
+                nc.vector.tensor_scalar(result[:], bank[:], bias[:, 0:1], 0.0, ADD, MAX)
+                nc.sync.dma_start(out[:, e * PIECE : (e + 1) * PIECE], result[:])
+            else:
+                nc.scalar.activation(result[:], bank[:], RELU, bias=bias[:, 0:1])
+                nc.scalar.dma_start(out[:, e * PIECE : (e + 1) * PIECE], result[:])

@@ -7,12 +7,16 @@ RELU = mybir.ActivationFunctionType.Relu
 
 P = 128
 TOKENS = 1024
-BLOCKS = TOKENS // P
 EXPERTS = 4
 PIECE = 512
-PIECE_COLS = PIECE // 16
-HALF = TOKENS // 2
-
+PART = 256
+PARTS = EXPERTS * PIECE // PART
+PART_COLS = PART // 16
+CHUNKS = 4
+CHUNK = TOKENS // CHUNKS
+BLOCKS = CHUNK // P
+WARM_UPS = 4
+FILLERS = 4
 FLOPS = 2 * P * P * EXPERTS * PIECE
 
 
@@ -20,15 +24,26 @@ def tile_gather_matmul_kernel(tc, table, w, b, offs, out):
     nc = tc.nc
     with (
         tc.tile_pool(name="held", bufs=1) as held,
-        tc.psum_pool(name="flip", bufs=1) as flip,
-        tc.psum_pool(name="product", bufs=1) as product,
+        tc.psum_pool(name="flip", bufs=CHUNKS) as flip,
+        tc.psum_pool(name="product", bufs=EXPERTS) as product,
     ):
-        offsets = held.tile([P, EXPERTS * PIECE_COLS], U16, name="offsets")
+        zeros = held.tile([P, P], BF16, name="zeros")
+        nc.vector.memset(zeros[:], 0.0)
+        zeros_repeated = zeros[:].unsqueeze(1).to_broadcast([P, PIECE // P, P])
+        unread = product.tile([P, PIECE // P, P], F32, tag="bank")
+        for i in range(WARM_UPS):
+            nc.tensor.matmul(unread[:], zeros[:], zeros_repeated, start=True, stop=True)
+
+        rows = []
+        for c in range(CHUNKS):
+            rows.append(held.tile([P, BLOCKS, P], BF16, name=f"rows{c}"))
+            chunk = table[c * CHUNK : (c + 1) * CHUNK, :]
+            queue = nc.sync if c % 2 == 0 else nc.scalar
+            queue.dma_start(rows[c][:], chunk.rearrange("(a p) k -> p a k", p=P))
+        offsets = held.tile([P, PARTS * PART_COLS], U16, name="offsets")
         nc.sync.dma_start(offsets[:], offs)
-        rows = held.tile([P, BLOCKS, P], BF16, name="rows")
-        nc.scalar.dma_start(rows[:], table.rearrange("(a p) k -> p a k", p=P))
         weights = held.tile([P, EXPERTS, P], BF16, name="weights")
-        nc.sync.dma_start(weights[:], w.rearrange("e k m -> k e m"))
+        nc.scalar.dma_start(weights[:], w.rearrange("e k m -> k e m"))
         bias = held.tile([P, 1], F32, name="bias")
         nc.sync.dma_start(bias[:], b)
 
@@ -36,21 +51,27 @@ def tile_gather_matmul_kernel(tc, table, w, b, offs, out):
         make_identity(nc, identity[:])
 
         window = held.tile([P, TOKENS], BF16, name="window")
-        flipped = [flip.tile([P, HALF], BF16, name=f"flipped{h}") for h in range(2)]
-        for a in range(BLOCKS):
-            h, col = divmod(a * P, HALF)
-            nc.tensor.transpose(flipped[h][:, col : col + P], rows[:, a, :], identity[:])
-        nc.vector.tensor_copy(window[:, 0:HALF], flipped[0][:])
-        nc.scalar.copy(window[:, HALF:TOKENS], flipped[1][:])
+        for c in range(CHUNKS):
+            flipped = flip.tile([P, CHUNK], BF16, name="flipped")
+            for a in range(BLOCKS):
+                nc.tensor.transpose(flipped[:, a * P : (a + 1) * P], rows[c][:, a, :], identity[:])
+            if c % 2 == 0:
+                nc.vector.tensor_copy(window[:, c * CHUNK : (c + 1) * CHUNK], flipped[:])
+            else:
+                nc.scalar.copy(window[:, c * CHUNK : (c + 1) * CHUNK], flipped[:])
 
-        for e in range(EXPERTS):
-            bank = product.tile([P, PIECE], F32, name=f"bank{e}")
-            picked = window[:].indirect(offsets[:, e * PIECE_COLS : (e + 1) * PIECE_COLS])
+        for i in range(FILLERS):
+            nc.tensor.matmul(unread[:, 0:BLOCKS, :], zeros[:], rows[CHUNKS - 1][:], start=True, stop=True)
+
+        for j in range(PARTS):
+            e = j * PART // PIECE
+            bank = product.tile([P, PART], F32, tag="bank")
+            picked = window[:].indirect(offsets[:, j * PART_COLS : (j + 1) * PART_COLS])
             nc.tensor.matmul(bank[:], weights[:, e, :], picked, start=True, stop=True)
-            result = held.tile([P, PIECE], F32, name=f"result{e}")
-            if e % 2 == 0:
+            result = held.tile([P, PART], F32, name=f"result{j}")
+            if j % 2 == 0:
                 nc.vector.tensor_scalar(result[:], bank[:], bias[:, 0:1], 0.0, ADD, MAX)
-                nc.sync.dma_start(out[:, e * PIECE : (e + 1) * PIECE], result[:])
+                nc.sync.dma_start(out[:, j * PART : (j + 1) * PART], result[:])
             else:
                 nc.scalar.activation(result[:], bank[:], RELU, bias=bias[:, 0:1])
-                nc.scalar.dma_start(out[:, e * PIECE : (e + 1) * PIECE], result[:])
+                nc.scalar.dma_start(out[:, j * PART : (j + 1) * PART], result[:])

@@ -15,8 +15,7 @@ PART_COLS = PART // 16
 CHUNKS = 4
 CHUNK = TOKENS // CHUNKS
 BLOCKS = CHUNK // P
-WARM_UPS = 4
-FILLERS = 4
+
 FLOPS = 2 * P * P * EXPERTS * PIECE
 
 
@@ -27,13 +26,6 @@ def tile_gather_matmul_kernel(tc, table, w, b, offs, out):
         tc.psum_pool(name="flip", bufs=CHUNKS) as flip,
         tc.psum_pool(name="product", bufs=EXPERTS) as product,
     ):
-        zeros = held.tile([P, P], BF16, name="zeros")
-        nc.vector.memset(zeros[:], 0.0)
-        zeros_repeated = zeros[:].unsqueeze(1).to_broadcast([P, PIECE // P, P])
-        unread = product.tile([P, PIECE // P, P], F32, tag="bank")
-        for i in range(WARM_UPS):
-            nc.tensor.matmul(unread[:], zeros[:], zeros_repeated, start=True, stop=True)
-
         rows = []
         for c in range(CHUNKS):
             rows.append(held.tile([P, BLOCKS, P], BF16, name=f"rows{c}"))
@@ -59,9 +51,6 @@ def tile_gather_matmul_kernel(tc, table, w, b, offs, out):
                 nc.vector.tensor_copy(window[:, c * CHUNK : (c + 1) * CHUNK], flipped[:])
             else:
                 nc.scalar.copy(window[:, c * CHUNK : (c + 1) * CHUNK], flipped[:])
-
-        for i in range(FILLERS):
-            nc.tensor.matmul(unread[:, 0:BLOCKS, :], zeros[:], rows[CHUNKS - 1][:], start=True, stop=True)
 
         for j in range(PARTS):
             e = j * PART // PIECE

@@ -15,6 +15,7 @@ PART_COLS = PART // 16
 CHUNKS = 4
 CHUNK = TOKENS // CHUNKS
 BLOCKS = CHUNK // P
+WARMUPS = 4
 
 FLOPS = 2 * P * P * EXPERTS * PIECE
 
@@ -38,6 +39,13 @@ def tile_gather_matmul_kernel(tc, table, w, b, offs, out):
         nc.scalar.dma_start(weights[:], w.rearrange("e k m -> k e m"))
         bias = held.tile([P, 1], F32, name="bias")
         nc.sync.dma_start(bias[:], b)
+
+        zeros = held.tile([P, P], BF16, name="zeros")
+        nc.vector.memset(zeros[:], 0.0)
+        unread = product.tile([P, PIECE], F32, tag="bank")
+        for i in range(WARMUPS):
+            repeated = zeros[:].unsqueeze(1).to_broadcast([P, PIECE // P, P])
+            nc.tensor.matmul(unread[:], zeros[:], repeated, start=True, stop=True)
 
         identity = held.tile([P, P], BF16, name="identity")
         make_identity(nc, identity[:])

@@ -36,7 +36,8 @@ def tile_gather_matmul_kernel(tc, table, w, b, offs, out):
         offsets = held.tile([P, PARTS * PART_COLS], U16, name="offsets")
         nc.sync.dma_start(offsets[:], offs)
         weights = held.tile([P, EXPERTS, P], BF16, name="weights")
-        nc.scalar.dma_start(weights[:], w.rearrange("e k m -> k e m"))
+        for e in range(0, EXPERTS, 2):
+            nc.scalar.dma_start(weights[:, e : e + 2, :], w[e : e + 2].rearrange("e k m -> k e m"))
         bias = held.tile([P, 1], F32, name="bias")
         nc.sync.dma_start(bias[:], b)
 

import concourse.mybir as mybir
from concourse.masks import make_identity

BF16, F32, U16 = mybir.dt.bfloat16, mybir.dt.float32, mybir.dt.uint16
ADD, MAX = mybir.AluOpType.add, mybir.AluOpType.max
RELU = mybir.ActivationFunctionType.Relu

P = 128
TOKENS = 1024
EXPERTS = 4
PIECE = 512
PART = 256
PARTS = EXPERTS * PIECE // PART
PART_COLS = PART // 16
CHUNKS = 4
CHUNK = TOKENS // CHUNKS
BLOCKS = CHUNK // P
WARMUPS = 4

FLOPS = 2 * P * P * EXPERTS * PIECE


def tile_gather_matmul_kernel(tc, table, w, b, offs, out):
    nc = tc.nc
    with (
        tc.tile_pool(name="held", bufs=1) as held,
        tc.psum_pool(name="flip", bufs=CHUNKS) as flip,
        tc.psum_pool(name="product", bufs=EXPERTS) as product,
    ):
        rows = []
        for c in range(CHUNKS):
            rows.append(held.tile([P, BLOCKS, P], BF16, name=f"rows{c}"))
            chunk = table[c * CHUNK : (c + 1) * CHUNK, :]
            queue = nc.sync if c % 2 == 0 else nc.scalar
            queue.dma_start(rows[c][:], chunk.rearrange("(a p) k -> p a k", p=P))
        offsets = held.tile([P, PARTS * PART_COLS], U16, name="offsets")
        nc.sync.dma_start(offsets[:], offs)
        weights = held.tile([P, EXPERTS, P], BF16, name="weights")
        for e in range(0, EXPERTS, 2):
            nc.scalar.dma_start(weights[:, e : e + 2, :], w[e : e + 2].rearrange("e k m -> k e m"))
        bias = held.tile([P, 1], F32, name="bias")
        nc.sync.dma_start(bias[:], b)

        zeros = held.tile([P, P], BF16, name="zeros")
        nc.vector.memset(zeros[:], 0.0)
        unread = product.tile([P, PIECE], F32, tag="bank")
        for i in range(WARMUPS):
            repeated = zeros[:].unsqueeze(1).to_broadcast([P, PIECE // P, P])
            nc.tensor.matmul(unread[:], zeros[:], repeated, start=True, stop=True)

        identity = held.tile([P, P], BF16, name="identity")
        make_identity(nc, identity[:])

        window = held.tile([P, TOKENS], BF16, name="window")
        for c in range(CHUNKS):
            flipped = flip.tile([P, CHUNK], BF16, name="flipped")
            for a in range(BLOCKS):
                nc.tensor.transpose(flipped[:, a * P : (a + 1) * P], rows[c][:, a, :], identity[:])
            if c % 2 == 0:
                nc.vector.tensor_copy(window[:, c * CHUNK : (c + 1) * CHUNK], flipped[:])
            else:
                nc.scalar.copy(window[:, c * CHUNK : (c + 1) * CHUNK], flipped[:])

        for j in range(PARTS):
            e = j * PART // PIECE
            bank = product.tile([P, PART], F32, tag="bank")
            picked = window[:].indirect(offsets[:, j * PART_COLS : (j + 1) * PART_COLS])
            nc.tensor.matmul(bank[:], weights[:, e, :], picked, start=True, stop=True)
            result = held.tile([P, PART], F32, name=f"result{j}")
            if j % 2 == 0:
                nc.vector.tensor_scalar(result[:], bank[:], bias[:, 0:1], 0.0, ADD, MAX)
                nc.sync.dma_start(out[:, j * PART : (j + 1) * PART], result[:])
            else:
                nc.scalar.activation(result[:], bank[:], RELU, bias=bias[:, 0:1])
                nc.scalar.dma_start(out[:, j * PART : (j + 1) * PART], result[:])
